import numpy as np
import ml_dtypes


def mxq(x, axis, fmt="e4m3"):
    dtype, down = {"e4m3": (ml_dtypes.float8_e4m3fn, 7), "e5m2": (ml_dtypes.float8_e5m2, 14)}[fmt]
    v = np.moveaxis(np.asarray(x, np.float32).astype(ml_dtypes.bfloat16).astype(np.float64), axis, -1)
    blocks = v.reshape(v.shape[:-1] + (-1, 32))
    amax = np.abs(blocks).max(-1, keepdims=True)
    byte = np.maximum(np.where(amax > 0, np.frexp(amax)[1] - 1 + 127, 0) - down, 1)
    scale = np.exp2(byte - 127.0)
    codes = (blocks / scale).astype(np.float32).astype(dtype).astype(np.float64)
    return np.moveaxis((codes * scale).reshape(v.shape), -1, axis)


WIDE = False


def mx_kscale(k):
    if not WIDE:
        return np.ones(k)
    levels = np.array([30, -30])
    if k % 512:
        return np.exp2(np.random.permutation(np.resize(levels, k // 32))).repeat(32)
    a = np.empty((k // 512, 16))
    for p in range(k // 512):
        a[p, :8] = np.random.permutation(np.resize(levels, 8))
        for g in range(8):
            far = levels[np.abs(levels - a[p, g]) >= 10]
            a[p, g + 8] = far[np.random.randint(len(far))]
    return np.exp2(a.ravel()).repeat(32)


def f64(x):
    return np.asarray(x).astype(np.float64)


def striped(idx):
    return np.tile(np.asarray(idx).reshape(-1, 16).T, (8, 1)).astype(np.uint16)


def unstriped(offs):
    return offs[:16].T.reshape(-1).astype(np.int64)


E2M1 = np.array([0.0, 0.5, 1.0, 1.5, 2.0, 3.0, 4.0, 6.0, -0.0, -0.5, -1.0, -1.5, -2.0, -3.0, -4.0, -6.0])


def pack_weight(w, fmt):
    k, n = w.shape
    w = f64(np.asarray(w, np.float32).astype(ml_dtypes.bfloat16)).reshape(k // 32, 32, n)
    amax = np.abs(w).max(1)
    if fmt == "e4m3":
        byte = np.frexp(amax)[1] - 1 + 127 - 7
    else:
        mant, ex = np.frexp(amax / 6.0)
        byte = np.where(mant > 0.5, ex, ex - 1) + 127
    byte = np.clip(np.where(amax > 0, byte, 1), 1, 254)
    scaled = (w * np.exp2(127.0 - byte)[:, None, :]).reshape(k, n).astype(np.float32)
    by_word = np.ascontiguousarray(scaled.reshape(k // 512, 128, 4, n).transpose(0, 1, 3, 2))
    if fmt == "e4m3":
        words = by_word.astype(ml_dtypes.float8_e4m3fn).view(np.uint8)
    else:
        c = by_word.astype(ml_dtypes.float4_e2m1fn).view(np.uint8) & 0xF
        words = (c[..., 0::2] | (c[..., 1::2] << 4)).reshape(k // 512, 128, 2 * n)
    return np.ascontiguousarray(words), np.ascontiguousarray(byte.astype(np.uint8).reshape(k // 512, 16, n))


def unpack_weight(words, scales, fmt):
    g, _, n = scales.shape
    words = np.ascontiguousarray(words).reshape(g, 128, n, -1)
    if fmt == "e4m3":
        vals = words.view(ml_dtypes.float8_e4m3fn).astype(np.float64)
    else:
        nib = np.empty((g, 128, n, 4), np.uint8)
        nib[..., 0::2] = words & 0xF
        nib[..., 1::2] = words >> 4
        vals = E2M1[nib]
    vals = vals * np.repeat(np.exp2(scales.astype(np.float64) - 127.0), 8, axis=1)[..., None]
    return vals.transpose(0, 1, 3, 2).reshape(g * 512, n)


K, J, N, R, T, V, Q = 512, 512, 256, 256, 1024, 1024, 64


def setup_inputs():
    n = np.random.standard_normal
    idx = np.random.permutation(T)[:J]
    idx2 = np.random.permutation(T)[:J]
    idx3 = np.random.permutation(V)[:J]
    idx4 = np.random.permutation(V)[:J]
    fj = mx_kscale(J)
    fk = mx_kscale(K)
    drp = pack_weight(n((K, R)) * 1 / np.sqrt(K) / fk[:, None], "e2m1")
    return {
        "xf": (n((K, T))).astype(np.float32),
        "ra": (np.random.uniform(0.5, 1.5, (1, J)) * fj).astype(np.float32),
        "gt": (n((N, V)) * np.exp(0.5 * n((1, V)))).astype(np.float32),
        "rb": (np.random.uniform(0.5, 1.5, (1, J)) / fj).astype(np.float32),
        "fkr": (np.random.uniform(0.5, 1.5, (1, K)) * fk).astype(np.float32),
        "dr_words": drp[0],
        "dr_scales": drp[1],
        "gr1c": (np.random.uniform(0.5, 2.0, (R, 1))).astype(np.float32),
        "offs": striped(idx),
        "offs2": striped(idx2),
        "offs3": striped(idx3),
        "offs4": striped(idx4),
    }


def reference(xf, ra, gt, rb, fkr, dr_words, dr_scales, gr1c, offs, offs2, offs3, offs4):
    idx = unstriped(offs)
    idx2 = unstriped(offs2)
    idx3 = unstriped(offs3)
    idx4 = unstriped(offs4)
    dru = unpack_weight(dr_words, dr_scales, "e2m1")
    us = (f64(xf)[:, idx] - f64(xf)[:, idx2]) * f64(ra)
    ut = us.T
    uj = ut * f64(fkr)
    gs = (f64(gt)[:, idx3] - 0.7 * f64(gt)[:, idx4]) * f64(rb)
    gj = gs.T
    ujq = mxq(uj, 0, "e5m2")
    gjq = mxq(gj, 0, "e5m2")
    w = ujq.T @ gjq
    wq = mxq(w, 0, "e5m2")
    v2 = dru.T @ wq
    wq = v2.reshape(R, Q, N // Q).sum(axis=2)
    y = 0.02 * wq * f64(gr1c)
    return y

@@ -1,0 +1,249 @@
+from contextlib import ExitStack
+
+import concourse.mybir as mybir
+from concourse.masks import make_identity
+
+K, J, N, R, T, V, Q = 512, 512, 256, 256, 1024, 1024, 64
+FLOPS = 2 * K * J * N + 2 * R * K * N
+
+F32 = mybir.dt.float32
+BF16 = mybir.dt.bfloat16
+I32 = mybir.dt.int32
+U32 = mybir.dt.uint32
+U16 = mybir.dt.uint16
+U8 = mybir.dt.uint8
+E5M2X4 = mybir.dt.float8_e5m2_x4
+E2M1X4 = mybir.dt.float4_e2m1fn_x4
+ALU = mybir.AluOpType
+COPY = mybir.ActivationFunctionType.Copy
+
+P = 128
+PACK = 4
+LIST_COLS = J // 16
+
+
+def tile_list_directions_gaps_differences_sums_kernel(
+    tc, xf, ra, gt, rb, fkr, dr_words, dr_scales, gr1c, offs, offs2, offs3, offs4, out
+):
+    nc = tc.nc
+    with ExitStack() as ctx:
+        sb = ctx.enter_context(tc.tile_pool(name="sb", bufs=1))
+        ps = ctx.enter_context(tc.psum_pool(name="ps", bufs=1))
+
+        def sbuf(name, shape, dtype):
+            return sb.tile(shape, dtype, name=name, align_bytes=64)
+
+        idx_a = sbuf("idx_a", [P, LIST_COLS], U16)
+        idx_b = sbuf("idx_b", [P, LIST_COLS], U16)
+        idx_c = sbuf("idx_c", [P, LIST_COLS], U16)
+        idx_d = sbuf("idx_d", [P, LIST_COLS], U16)
+        x_win = [sbuf(f"x_win{t}", [P, T], F32) for t in range(PACK)]
+        g_win = [sbuf(f"g_win{h}", [P, V], F32) for h in range(2)]
+        ra_col = sbuf("ra_col", [P, PACK], F32)
+        rb_col = sbuf("rb_col", [P, PACK], F32)
+        fk_col = sbuf("fk_col", [P, PACK], F32)
+        gr_col = sbuf("gr_col", [P, 2], F32)
+        dr_codes = sbuf("dr_codes", [P, 2 * R], U8)
+        dr_scale = sbuf("dr_scale", [P, R], U8)
+        ident = sbuf("ident", [P, P], F32)
+
+        x_rows = xf.rearrange("(p t) v -> t p v", t=PACK)
+        g_rows = gt.rearrange("(m h) v -> h m v", h=2)
+
+        def by_four(vec):
+            return vec.rearrange("o (p t) -> (o p) t", t=PACK)
+
+        with nc.allow_non_contiguous_dma(reason="one factor for each partition and half"):
+            nc.scalar.dma_start(out=gr_col[:], in_=gr1c.rearrange("(h p) o -> p (h o)", h=2))
+        nc.scalar.dma_start(out=ra_col[:], in_=by_four(ra))
+        nc.sync.dma_start(idx_d[:], offs4)
+        nc.sync.dma_start(idx_c[:], offs3)
+        nc.sync.dma_start(out=g_win[0][:], in_=g_rows[0])
+        nc.sync.dma_start(out=x_win[0][:], in_=x_rows[0])
+        nc.sync.dma_start(idx_b[:], offs2)
+        nc.sync.dma_start(idx_a[:], offs)
+        nc.sync.dma_start(out=fk_col[:], in_=by_four(fkr))
+        nc.sync.dma_start(out=rb_col[:], in_=by_four(rb))
+        nc.sync.dma_start(out=x_win[1][:], in_=x_rows[1])
+        nc.sync.dma_start(out=g_win[1][:], in_=g_rows[1])
+        nc.sync.dma_start(out=x_win[2][:], in_=x_rows[2])
+        nc.sync.dma_start(out=x_win[3][:], in_=x_rows[3])
+        nc.gpsimd.memset(dr_scale[:].bitcast(I32), 0)
+        make_identity(nc, ident[:])
+        nc.sync.dma_start(out=dr_codes[:].bitcast(I32), in_=dr_words[0].bitcast(I32))
+        for quad in range(4):
+            nc.sync.dma_start(
+                out=dr_scale[32 * quad : 32 * quad + 4, :].bitcast(I32),
+                in_=dr_scales[0, 4 * quad : 4 * quad + 4, :].bitcast(I32),
+            )
+
+        out_factor = sbuf("out_factor", [P, 2], F32)
+        nc.scalar.activation(out_factor[:], gr_col[:], COPY, scale=0.02)
+
+        ra_bank = ps.tile([P, PACK, P], F32, name="ra_bank")
+        g_bank = [ps.tile([P, PACK, P], F32, name=f"g_bank{h}") for h in range(2)]
+        u_bank = [ps.tile([P, 2, P], F32, name=f"u_bank{i}") for i in range(2)]
+        w_bank = [ps.tile([P, PACK, P], F32, name=f"w_bank{h}") for h in range(2)]
+        v_bank = ps.tile([P, 2, P], F32, name="v_bank")
+
+        x_second = [sbuf(f"x_second{t}", [P, J], F32) for t in range(PACK)]
+        x_diff = [sbuf(f"x_diff{t}", [P, J], F32) for t in range(PACK)]
+        u_rows = [sbuf(f"u_rows{t}", [P, J], BF16) for t in range(PACK)]
+        u_in = [sbuf(f"u_in{t}", [P, PACK * P], BF16) for t in range(PACK)]
+        u_codes = [sbuf(f"u_codes{t}", [P, P], U32) for t in range(PACK)]
+        u_scale = [sbuf(f"u_scale{t}", [P, P], U8) for t in range(PACK)]
+        g_first = [sbuf(f"g_first{h}", [P, J], F32) for h in range(2)]
+        g_second = [sbuf(f"g_second{h}", [P, J], F32) for h in range(2)]
+        g_in = [sbuf(f"g_in{h}", [P, PACK * P], BF16) for h in range(2)]
+        g_codes = [sbuf(f"g_codes{h}", [P, P], U32) for h in range(2)]
+        g_scale = [sbuf(f"g_scale{h}", [P, P], U8) for h in range(2)]
+        w_in = [sbuf(f"w_in{h}", [P, PACK * P], BF16) for h in range(2)]
+        w_codes = [sbuf(f"w_codes{h}", [P, P], U32) for h in range(2)]
+        w_scale = [sbuf(f"w_scale{h}", [P, P], U8) for h in range(2)]
+        sums = sbuf("sums", [P, 2, Q], F32)
+        result = sbuf("result", [P, 2, Q], F32)
+
+        def pieces(count):
+            width = J // count
+            return [
+                (slice(i * width, (i + 1) * width), slice(i * width // 16, (i + 1) * width // 16))
+                for i in range(count)
+            ]
+
+        def quantize(codes, scale, values):
+            nc.vector.quantize_mx(out=codes[:].bitcast(E5M2X4), scales=scale[:], in_=values[:])
+
+        def spread_ra():
+            for t in range(PACK):
+                nc.tensor.transpose(ra_bank[:, t, :], ra_col[:, t : t + 1].to_broadcast([P, P]), ident[:])
+
+        def x_gather_second(t, count):
+            for cols, offsets in pieces(count):
+                nc.scalar.activation(x_second[t][:, cols], x_win[t][:].indirect(idx_b[:, offsets]), COPY)
+
+        def x_gather_subtract(t, count):
+            for cols, offsets in pieces(count):
+                nc.vector.tensor_tensor(
+                    x_diff[t][:, cols], x_win[t][:].indirect(idx_a[:, offsets]), x_second[t][:, cols], ALU.subtract
+                )
+
+        def x_weigh(t, count):
+            ra_by_j = ra_bank[:].rearrange("p t m -> p m t")
+            width = P // count
+            for i in range(count):
+                cols = slice(PACK * width * i, PACK * width * (i + 1))
+                nc.vector.scalar_tensor_tensor(
+                    out=u_rows[t][:, cols].rearrange("p (m t) -> p m t", t=PACK),
+                    in0=x_diff[t][:, cols].rearrange("p (m t) -> p m t", t=PACK),
+                    scalar=fk_col[:, t : t + 1],
+                    in1=ra_by_j[:, width * i : width * (i + 1), :],
+                    op0=ALU.mult,
+                    op1=ALU.mult,
+                )
+
+        def x_turn(t):
+            words = u_rows[t][:].bitcast(F32)
+            bank = u_bank[t % 2]
+            for u in range(2):
+                nc.tensor.transpose(bank[:, u, :], words[:, u::2], ident[:])
+            nc.scalar.copy(
+                out=u_in[t][:].bitcast(F32).rearrange("p (m u) -> p m u", u=2),
+                in_=bank[:].rearrange("p u m -> p m u"),
+            )
+
+        def g_turn(h, picked, first):
+            for t in range(PACK):
+                nc.tensor.matmul(
+                    g_bank[h][:, t, :],
+                    lhsT=picked[:, t::PACK],
+                    rhs=ident[:],
+                    is_transpose=True,
+                    start=(first and t == 0),
+                    stop=(not first and t == PACK - 1),
+                )
+
+        def g_gather_second(h):
+            nc.scalar.activation(g_second[h][:], g_win[h][:].indirect(idx_d[:]), COPY, scale=-0.7)
+            g_turn(h, g_second[h], True)
+
+        def g_weigh(h):
+            nc.vector.tensor_tensor(
+                g_in[h][:].rearrange("p (m t) -> p m t", t=PACK),
+                g_bank[h][:].rearrange("p t m -> p m t"),
+                rb_col[:].unsqueeze(1).to_broadcast([P, P, PACK]),
+                ALU.mult,
+            )
+
+        def moment(t, h):
+            nc.tensor.matmul_mx(
+                out=w_bank[h][:, t, :],
+                lhsT=u_codes[t][:].bitcast(E5M2X4),
+                lhsT_scale=u_scale[t][:],
+                rhs=g_codes[h][:].bitcast(E5M2X4),
+                rhs_scale=g_scale[h][:],
+                start=True,
+                stop=True,
+            )
+
+        g_gather_second(0)
+        nc.vector.tensor_copy(g_first[0][:], g_win[0][:].indirect(idx_c[:]))
+        g_turn(0, g_first[0], False)
+        spread_ra()
+        x_gather_second(0, 4)
+        x_gather_subtract(0, 4)
+        x_gather_second(1, 1)
+        x_weigh(0, 1)
+        g_weigh(0)
+        g_gather_second(1)
+        x_turn(0)
+        x_gather_subtract(1, 1)
+        x_weigh(1, 1)
+        x_gather_second(2, 2)
+        quantize(g_codes[0], g_scale[0], g_in[0])
+        quantize(u_codes[0], u_scale[0], u_in[0])
+        nc.scalar.activation(g_first[1][:], g_win[1][:].indirect(idx_c[:]), COPY)
+        g_turn(1, g_first[1], False)
+        x_turn(1)
+        x_gather_subtract(2, 2)
+        x_weigh(2, 1)
+        x_gather_second(3, 1)
+        quantize(u_codes[1], u_scale[1], u_in[1])
+        g_weigh(1)
+        x_turn(2)
+        x_gather_subtract(3, 2)
+        x_weigh(3, 2)
+        quantize(g_codes[1], g_scale[1], g_in[1])
+        quantize(u_codes[2], u_scale[2], u_in[2])
+        x_turn(3)
+        for t in range(PACK - 1):
+            for h in range(2):
+                moment(t, h)
+        quantize(u_codes[3], u_scale[3], u_in[3])
+        for h in range(2):
+            moment(PACK - 1, h)
+
+        nc.scalar.copy(out=w_in[0][:].rearrange("p (m t) -> p m t", t=PACK), in_=w_bank[0][:].rearrange("p t m -> p m t"))
+        nc.vector.tensor_copy(out=w_in[1][:].rearrange("p (m t) -> p m t", t=PACK), in_=w_bank[1][:].rearrange("p t m -> p m t"))
+        for h in range(2):
+            quantize(w_codes[h], w_scale[h], w_in[h])
+        for h in range(2):
+            for half in range(2):
+                nc.tensor.matmul_mx(
+                    out=v_bank[:, half, :],
+                    lhsT=dr_codes[:, 2 * P * half : 2 * P * (half + 1)].bitcast(E2M1X4),
+                    lhsT_scale=dr_scale[:, P * half : P * (half + 1)],
+                    rhs=w_codes[h][:].bitcast(E5M2X4),
+                    rhs_scale=w_scale[h][:],
+                    start=(h == 0 and half == 0),
+                    stop=(h == 1 and half == 1),
+                )
+        nc.vector.tensor_reduce(
+            out=sums[:].rearrange("p a q -> p (a q)"),
+            in_=v_bank[:].rearrange("p a (q e) -> p (a q) e", e=2),
+            axis=mybir.AxisListType.X,
+            op=ALU.add,
+        )
+        nc.vector.tensor_tensor(
+            result[:], sums[:], out_factor[:].unsqueeze(2).to_broadcast([P, 2, Q]), ALU.mult
+        )
+        nc.sync.dma_start(out=out.rearrange("(a p) q -> p a q", a=2), in_=result[:])

@@ -53,23 +53,23 @@ def tile_list_directions_gaps_differences_sums_kernel(
         def by_four(vec):
             return vec.rearrange("o (p t) -> (o p) t", t=PACK)
 
-        with nc.allow_non_contiguous_dma(reason="one factor for each partition and half"):
-            nc.scalar.dma_start(out=gr_col[:], in_=gr1c.rearrange("(h p) o -> p (h o)", h=2))
-        nc.scalar.dma_start(out=ra_col[:], in_=by_four(ra))
+        nc.sync.dma_start(out=g_win[0][:], in_=g_rows[0])
         nc.sync.dma_start(idx_d[:], offs4)
         nc.sync.dma_start(idx_c[:], offs3)
-        nc.sync.dma_start(out=g_win[0][:], in_=g_rows[0])
         nc.sync.dma_start(out=x_win[0][:], in_=x_rows[0])
         nc.sync.dma_start(idx_b[:], offs2)
         nc.sync.dma_start(idx_a[:], offs)
+        nc.sync.dma_start(out=ra_col[:], in_=by_four(ra))
         nc.sync.dma_start(out=fk_col[:], in_=by_four(fkr))
         nc.sync.dma_start(out=rb_col[:], in_=by_four(rb))
         nc.sync.dma_start(out=x_win[1][:], in_=x_rows[1])
-        nc.sync.dma_start(out=g_win[1][:], in_=g_rows[1])
         nc.sync.dma_start(out=x_win[2][:], in_=x_rows[2])
+        nc.sync.dma_start(out=g_win[1][:], in_=g_rows[1])
         nc.sync.dma_start(out=x_win[3][:], in_=x_rows[3])
-        nc.gpsimd.memset(dr_scale[:].bitcast(I32), 0)
+        with nc.allow_non_contiguous_dma(reason="one factor for each partition and half"):
+            nc.sync.dma_start(out=gr_col[:], in_=gr1c.rearrange("(h p) o -> p (h o)", h=2))
         make_identity(nc, ident[:])
+        nc.gpsimd.memset(dr_scale[:].bitcast(I32), 0)
         nc.sync.dma_start(out=dr_codes[:].bitcast(I32), in_=dr_words[0].bitcast(I32))
         for quad in range(4):
             nc.sync.dma_start(
@@ -77,24 +77,27 @@ def tile_list_directions_gaps_differences_sums_kernel(
                 in_=dr_scales[0, 4 * quad : 4 * quad + 4, :].bitcast(I32),
             )
 
-        out_factor = sbuf("out_factor", [P, 2], F32)
-        nc.scalar.activation(out_factor[:], gr_col[:], COPY, scale=0.02)
+        warm_in = sbuf("warm_in", [P, 1], F32)
+        warm_out = sbuf("warm_out", [P, 1], F32)
+        nc.vector.memset(warm_in[:], 0.0)
+        nc.scalar.activation(warm_out[:], warm_in[:], COPY)
 
         ra_bank = ps.tile([P, PACK, P], F32, name="ra_bank")
         g_bank = [ps.tile([P, PACK, P], F32, name=f"g_bank{h}") for h in range(2)]
-        u_bank = [ps.tile([P, 2, P], F32, name=f"u_bank{i}") for i in range(2)]
+        u_bank = ps.tile([P, 2, 2, P], F32, name="u_bank")
         w_bank = [ps.tile([P, PACK, P], F32, name=f"w_bank{h}") for h in range(2)]
-        v_bank = ps.tile([P, 2, P], F32, name="v_bank")
+        v_first = ps.tile([P, P], F32, name="v_first")
+        v_bank = [v_first[:], g_bank[0][:, 0, :]]
 
         x_second = [sbuf(f"x_second{t}", [P, J], F32) for t in range(PACK)]
         x_diff = [sbuf(f"x_diff{t}", [P, J], F32) for t in range(PACK)]
         u_rows = [sbuf(f"u_rows{t}", [P, J], BF16) for t in range(PACK)]
-        u_in = [sbuf(f"u_in{t}", [P, PACK * P], BF16) for t in range(PACK)]
-        u_codes = [sbuf(f"u_codes{t}", [P, P], U32) for t in range(PACK)]
-        u_scale = [sbuf(f"u_scale{t}", [P, P], U8) for t in range(PACK)]
+        u_late = [sbuf(f"u_late{t}", [P, J // 2], F32) for t in range(2)]
+        u_codes = sbuf("u_codes", [P, K], U32)
+        u_scale = sbuf("u_scale", [P, K], U8)
         g_first = [sbuf(f"g_first{h}", [P, J], F32) for h in range(2)]
         g_second = [sbuf(f"g_second{h}", [P, J], F32) for h in range(2)]
-        g_in = [sbuf(f"g_in{h}", [P, PACK * P], BF16) for h in range(2)]
+        g_in = [x_second[t][:, : J // 2].bitcast(BF16) for t in (0, 3)]
         g_codes = [sbuf(f"g_codes{h}", [P, P], U32) for h in range(2)]
         g_scale = [sbuf(f"g_scale{h}", [P, P], U8) for h in range(2)]
         w_in = [sbuf(f"w_in{h}", [P, PACK * P], BF16) for h in range(2)]
@@ -111,7 +114,7 @@ def tile_list_directions_gaps_differences_sums_kernel(
             ]
 
         def quantize(codes, scale, values):
-            nc.vector.quantize_mx(out=codes[:].bitcast(E5M2X4), scales=scale[:], in_=values[:])
+            nc.vector.quantize_mx(out=codes.bitcast(E5M2X4), scales=scale, in_=values)
 
         def spread_ra():
             for t in range(PACK):
@@ -127,10 +130,10 @@ def tile_list_directions_gaps_differences_sums_kernel(
                     x_diff[t][:, cols], x_win[t][:].indirect(idx_a[:, offsets]), x_second[t][:, cols], ALU.subtract
                 )
 
-        def x_weigh(t, count):
+        def x_weigh(t, count, which=None):
             ra_by_j = ra_bank[:].rearrange("p t m -> p m t")
             width = P // count
-            for i in range(count):
+            for i in range(count) if which is None else [which]:
                 cols = slice(PACK * width * i, PACK * width * (i + 1))
                 nc.vector.scalar_tensor_tensor(
                     out=u_rows[t][:, cols].rearrange("p (m t) -> p m t", t=PACK),
@@ -141,15 +144,20 @@ def tile_list_directions_gaps_differences_sums_kernel(
                     op1=ALU.mult,
                 )
 
-        def x_turn(t):
+        def x_turn(t, bank):
             words = u_rows[t][:].bitcast(F32)
-            bank = u_bank[t % 2]
             for u in range(2):
                 nc.tensor.transpose(bank[:, u, :], words[:, u::2], ident[:])
+
+        def x_collect(words, banked):
             nc.scalar.copy(
-                out=u_in[t][:].bitcast(F32).rearrange("p (m u) -> p m u", u=2),
-                in_=bank[:].rearrange("p u m -> p m u"),
+                out=words.rearrange("p (s m u) -> p s m u", m=P, u=2),
+                in_=banked.rearrange("p s u m -> p s m u"),
             )
+
+        def x_quantize(t0, t1, words):
+            cols = slice(P * t0, P * t1)
+            quantize(u_codes[:, cols], u_scale[:, cols], words.bitcast(BF16))
 
         def g_turn(h, picked, first):
             for t in range(PACK):
@@ -168,7 +176,7 @@ def tile_list_directions_gaps_differences_sums_kernel(
 
         def g_weigh(h):
             nc.vector.tensor_tensor(
-                g_in[h][:].rearrange("p (m t) -> p m t", t=PACK),
+                g_in[h].rearrange("p (m t) -> p m t", t=PACK),
                 g_bank[h][:].rearrange("p t m -> p m t"),
                 rb_col[:].unsqueeze(1).to_broadcast([P, P, PACK]),
                 ALU.mult,
@@ -177,8 +185,8 @@ def tile_list_directions_gaps_differences_sums_kernel(
         def moment(t, h):
             nc.tensor.matmul_mx(
                 out=w_bank[h][:, t, :],
-                lhsT=u_codes[t][:].bitcast(E5M2X4),
-                lhsT_scale=u_scale[t][:],
+                lhsT=u_codes[:, P * t : P * (t + 1)].bitcast(E5M2X4),
+                lhsT_scale=u_scale[:, P * t : P * (t + 1)],
                 rhs=g_codes[h][:].bitcast(E5M2X4),
                 rhs_scale=g_scale[h][:],
                 start=True,
@@ -194,56 +202,58 @@ def tile_list_directions_gaps_differences_sums_kernel(
         x_gather_second(1, 1)
         x_weigh(0, 1)
         g_weigh(0)
-        g_gather_second(1)
-        x_turn(0)
+        x_turn(0, u_bank[:, 0])
         x_gather_subtract(1, 1)
+        x_gather_second(2, 1)
+        quantize(g_codes[0][:], g_scale[0][:], g_in[0])
         x_weigh(1, 1)
-        x_gather_second(2, 2)
-        quantize(g_codes[0], g_scale[0], g_in[0])
-        quantize(u_codes[0], u_scale[0], u_in[0])
+        x_turn(1, u_bank[:, 1])
+        g_gather_second(1)
         nc.scalar.activation(g_first[1][:], g_win[1][:].indirect(idx_c[:]), COPY)
         g_turn(1, g_first[1], False)
-        x_turn(1)
-        x_gather_subtract(2, 2)
+        x_gather_subtract(2, 1)
         x_weigh(2, 1)
-        x_gather_second(3, 1)
-        quantize(u_codes[1], u_scale[1], u_in[1])
-        g_weigh(1)
-        x_turn(2)
+        x_gather_second(3, 2)
+        x_collect(g_first[1][:], u_bank[:])
+        x_turn(2, u_bank[:, 0])
+        x_collect(u_late[0][:], u_bank[:, 0:1])
         x_gather_subtract(3, 2)
         x_weigh(3, 2)
-        quantize(g_codes[1], g_scale[1], g_in[1])
-        quantize(u_codes[2], u_scale[2], u_in[2])
-        x_turn(3)
-        for t in range(PACK - 1):
+        x_turn(3, u_bank[:, 1])
+        x_collect(u_late[1][:], u_bank[:, 1:2])
+        g_weigh(1)
+        x_quantize(0, 2, g_first[1][:])
+        quantize(g_codes[1][:], g_scale[1][:], g_in[1])
+        x_quantize(2, 3, u_late[0][:])
+        x_quantize(3, 4, u_late[1][:])
+        for t in range(PACK):
             for h in range(2):
                 moment(t, h)
-        quantize(u_codes[3], u_scale[3], u_in[3])
-        for h in range(2):
-            moment(PACK - 1, h)
 
         nc.scalar.copy(out=w_in[0][:].rearrange("p (m t) -> p m t", t=PACK), in_=w_bank[0][:].rearrange("p t m -> p m t"))
         nc.vector.tensor_copy(out=w_in[1][:].rearrange("p (m t) -> p m t", t=PACK), in_=w_bank[1][:].rearrange("p t m -> p m t"))
         for h in range(2):
-            quantize(w_codes[h], w_scale[h], w_in[h])
+            quantize(w_codes[h][:], w_scale[h][:], w_in[h][:])
         for h in range(2):
             for half in range(2):
                 nc.tensor.matmul_mx(
-                    out=v_bank[:, half, :],
+                    out=v_bank[half],
                     lhsT=dr_codes[:, 2 * P * half : 2 * P * (half + 1)].bitcast(E2M1X4),
                     lhsT_scale=dr_scale[:, P * half : P * (half + 1)],
                     rhs=w_codes[h][:].bitcast(E5M2X4),
                     rhs_scale=w_scale[h][:],
-                    start=(h == 0 and half == 0),
-                    stop=(h == 1 and half == 1),
+                    start=(h == 0),
+                    stop=(h == 1),
                 )
-        nc.vector.tensor_reduce(
-            out=sums[:].rearrange("p a q -> p (a q)"),
-            in_=v_bank[:].rearrange("p a (q e) -> p (a q) e", e=2),
-            axis=mybir.AxisListType.X,
-            op=ALU.add,
-        )
-        nc.vector.tensor_tensor(
-            result[:], sums[:], out_factor[:].unsqueeze(2).to_broadcast([P, 2, Q]), ALU.mult
-        )
+        for half in range(2):
+            nc.vector.tensor_reduce(
+                out=sums[:, half, :],
+                in_=v_bank[half].rearrange("p (q e) -> p q e", e=2),
+                axis=mybir.AxisListType.X,
+                op=ALU.add,
+            )
+        for half in range(2):
+            nc.vector.tensor_scalar(
+                result[:, half, :], sums[:, half, :], 0.02, gr_col[:, half : half + 1], ALU.mult, ALU.mult
+            )
         nc.sync.dma_start(out=out.rearrange("(a p) q -> p a q", a=2), in_=result[:])

from contextlib import ExitStack

import concourse.mybir as mybir
from concourse.masks import make_identity

K, J, N, R, T, V, Q = 512, 512, 256, 256, 1024, 1024, 64
FLOPS = 2 * K * J * N + 2 * R * K * N

F32 = mybir.dt.float32
BF16 = mybir.dt.bfloat16
I32 = mybir.dt.int32
U32 = mybir.dt.uint32
U16 = mybir.dt.uint16
U8 = mybir.dt.uint8
E5M2X4 = mybir.dt.float8_e5m2_x4
E2M1X4 = mybir.dt.float4_e2m1fn_x4
ALU = mybir.AluOpType
COPY = mybir.ActivationFunctionType.Copy

P = 128
PACK = 4
LIST_COLS = J // 16


def tile_list_directions_gaps_differences_sums_kernel(
    tc, xf, ra, gt, rb, fkr, dr_words, dr_scales, gr1c, offs, offs2, offs3, offs4, out
):
    nc = tc.nc
    with ExitStack() as ctx:
        sb = ctx.enter_context(tc.tile_pool(name="sb", bufs=1))
        ps = ctx.enter_context(tc.psum_pool(name="ps", bufs=1))

        def sbuf(name, shape, dtype):
            return sb.tile(shape, dtype, name=name, align_bytes=64)

        idx_a = sbuf("idx_a", [P, LIST_COLS], U16)
        idx_b = sbuf("idx_b", [P, LIST_COLS], U16)
        idx_c = sbuf("idx_c", [P, LIST_COLS], U16)
        idx_d = sbuf("idx_d", [P, LIST_COLS], U16)
        x_win = [sbuf(f"x_win{t}", [P, T], F32) for t in range(PACK)]
        g_win = [sbuf(f"g_win{h}", [P, V], F32) for h in range(2)]
        ra_col = sbuf("ra_col", [P, PACK], F32)
        rb_col = sbuf("rb_col", [P, PACK], F32)
        fk_col = sbuf("fk_col", [P, PACK], F32)
        gr_col = sbuf("gr_col", [P, 2], F32)
        dr_codes = sbuf("dr_codes", [P, 2 * R], U8)
        dr_scale = sbuf("dr_scale", [P, R], U8)
        ident = sbuf("ident", [P, P], F32)

        x_rows = xf.rearrange("(p t) v -> t p v", t=PACK)
        g_rows = gt.rearrange("(m h) v -> h m v", h=2)

        def by_four(vec):
            return vec.rearrange("o (p t) -> (o p) t", t=PACK)

        nc.sync.dma_start(out=g_win[0][:], in_=g_rows[0])
        nc.sync.dma_start(idx_d[:], offs4)
        nc.sync.dma_start(idx_c[:], offs3)
        nc.sync.dma_start(out=x_win[0][:], in_=x_rows[0])
        nc.sync.dma_start(idx_b[:], offs2)
        nc.sync.dma_start(idx_a[:], offs)
        nc.sync.dma_start(out=ra_col[:], in_=by_four(ra))
        nc.sync.dma_start(out=fk_col[:], in_=by_four(fkr))
        nc.sync.dma_start(out=rb_col[:], in_=by_four(rb))
        nc.sync.dma_start(out=x_win[1][:], in_=x_rows[1])
        nc.sync.dma_start(out=x_win[2][:], in_=x_rows[2])
        nc.sync.dma_start(out=g_win[1][:], in_=g_rows[1])
        nc.sync.dma_start(out=x_win[3][:], in_=x_rows[3])
        with nc.allow_non_contiguous_dma(reason="one factor for each partition and half"):
            nc.sync.dma_start(out=gr_col[:], in_=gr1c.rearrange("(h p) o -> p (h o)", h=2))
        make_identity(nc, ident[:])
        nc.gpsimd.memset(dr_scale[:].bitcast(I32), 0)
        nc.sync.dma_start(out=dr_codes[:].bitcast(I32), in_=dr_words[0].bitcast(I32))
        for quad in range(4):
            nc.sync.dma_start(
                out=dr_scale[32 * quad : 32 * quad + 4, :].bitcast(I32),
                in_=dr_scales[0, 4 * quad : 4 * quad + 4, :].bitcast(I32),
            )

        warm_in = sbuf("warm_in", [P, 1], F32)
        warm_out = sbuf("warm_out", [P, 1], F32)
        nc.vector.memset(warm_in[:], 0.0)
        nc.scalar.activation(warm_out[:], warm_in[:], COPY)

        ra_bank = ps.tile([P, PACK, P], F32, name="ra_bank")
        g_bank = [ps.tile([P, PACK, P], F32, name=f"g_bank{h}") for h in range(2)]
        u_bank = ps.tile([P, 2, 2, P], F32, name="u_bank")
        w_bank = [ps.tile([P, PACK, P], F32, name=f"w_bank{h}") for h in range(2)]
        v_first = ps.tile([P, P], F32, name="v_first")
        v_bank = [v_first[:], g_bank[0][:, 0, :]]

        x_second = [sbuf(f"x_second{t}", [P, J], F32) for t in range(PACK)]
        x_diff = [sbuf(f"x_diff{t}", [P, J], F32) for t in range(PACK)]
        u_rows = [sbuf(f"u_rows{t}", [P, J], BF16) for t in range(PACK)]
        u_late = [sbuf(f"u_late{t}", [P, J // 2], F32) for t in range(2)]
        u_codes = sbuf("u_codes", [P, K], U32)
        u_scale = sbuf("u_scale", [P, K], U8)
        g_first = [sbuf(f"g_first{h}", [P, J], F32) for h in range(2)]
        g_second = [sbuf(f"g_second{h}", [P, J], F32) for h in range(2)]
        g_in = [x_second[t][:, : J // 2].bitcast(BF16) for t in (0, 3)]
        g_codes = [sbuf(f"g_codes{h}", [P, P], U32) for h in range(2)]
        g_scale = [sbuf(f"g_scale{h}", [P, P], U8) for h in range(2)]
        w_in = [sbuf(f"w_in{h}", [P, PACK * P], BF16) for h in range(2)]
        w_codes = [sbuf(f"w_codes{h}", [P, P], U32) for h in range(2)]
        w_scale = [sbuf(f"w_scale{h}", [P, P], U8) for h in range(2)]
        sums = sbuf("sums", [P, 2, Q], F32)
        result = sbuf("result", [P, 2, Q], F32)

        def pieces(count):
            width = J // count
            return [
                (slice(i * width, (i + 1) * width), slice(i * width // 16, (i + 1) * width // 16))
                for i in range(count)
            ]

        def quantize(codes, scale, values):
            nc.vector.quantize_mx(out=codes.bitcast(E5M2X4), scales=scale, in_=values)

        def spread_ra():
            for t in range(PACK):
                nc.tensor.transpose(ra_bank[:, t, :], ra_col[:, t : t + 1].to_broadcast([P, P]), ident[:])

        def x_gather_second(t, count):
            for cols, offsets in pieces(count):
                nc.scalar.activation(x_second[t][:, cols], x_win[t][:].indirect(idx_b[:, offsets]), COPY)

        def x_gather_subtract(t, count):
            for cols, offsets in pieces(count):
                nc.vector.tensor_tensor(
                    x_diff[t][:, cols], x_win[t][:].indirect(idx_a[:, offsets]), x_second[t][:, cols], ALU.subtract
                )

        def x_weigh(t, count, which=None):
            ra_by_j = ra_bank[:].rearrange("p t m -> p m t")
            width = P // count
            for i in range(count) if which is None else [which]:
                cols = slice(PACK * width * i, PACK * width * (i + 1))
                nc.vector.scalar_tensor_tensor(
                    out=u_rows[t][:, cols].rearrange("p (m t) -> p m t", t=PACK),
                    in0=x_diff[t][:, cols].rearrange("p (m t) -> p m t", t=PACK),
                    scalar=fk_col[:, t : t + 1],
                    in1=ra_by_j[:, width * i : width * (i + 1), :],
                    op0=ALU.mult,
                    op1=ALU.mult,
                )

        def x_turn(t, bank):
            words = u_rows[t][:].bitcast(F32)
            for u in range(2):
                nc.tensor.transpose(bank[:, u, :], words[:, u::2], ident[:])

        def x_collect(words, banked):
            nc.scalar.copy(
                out=words.rearrange("p (s m u) -> p s m u", m=P, u=2),
                in_=banked.rearrange("p s u m -> p s m u"),
            )

        def x_quantize(t0, t1, words):
            cols = slice(P * t0, P * t1)
            quantize(u_codes[:, cols], u_scale[:, cols], words.bitcast(BF16))

        def g_turn(h, picked, first):
            for t in range(PACK):
                nc.tensor.matmul(
                    g_bank[h][:, t, :],
                    lhsT=picked[:, t::PACK],
                    rhs=ident[:],
                    is_transpose=True,
                    start=(first and t == 0),
                    stop=(not first and t == PACK - 1),
                )

        def g_gather_second(h):
            nc.scalar.activation(g_second[h][:], g_win[h][:].indirect(idx_d[:]), COPY, scale=-0.7)
            g_turn(h, g_second[h], True)

        def g_weigh(h):
            nc.vector.tensor_tensor(
                g_in[h].rearrange("p (m t) -> p m t", t=PACK),
                g_bank[h][:].rearrange("p t m -> p m t"),
                rb_col[:].unsqueeze(1).to_broadcast([P, P, PACK]),
                ALU.mult,
            )

        def moment(t, h):
            nc.tensor.matmul_mx(
                out=w_bank[h][:, t, :],
                lhsT=u_codes[:, P * t : P * (t + 1)].bitcast(E5M2X4),
                lhsT_scale=u_scale[:, P * t : P * (t + 1)],
                rhs=g_codes[h][:].bitcast(E5M2X4),
                rhs_scale=g_scale[h][:],
                start=True,
                stop=True,
            )

        g_gather_second(0)
        nc.vector.tensor_copy(g_first[0][:], g_win[0][:].indirect(idx_c[:]))
        g_turn(0, g_first[0], False)
        spread_ra()
        x_gather_second(0, 4)
        x_gather_subtract(0, 4)
        x_gather_second(1, 1)
        x_weigh(0, 1)
        g_weigh(0)
        x_turn(0, u_bank[:, 0])
        x_gather_subtract(1, 1)
        x_gather_second(2, 1)
        quantize(g_codes[0][:], g_scale[0][:], g_in[0])
        x_weigh(1, 1)
        x_turn(1, u_bank[:, 1])
        g_gather_second(1)
        nc.scalar.activation(g_first[1][:], g_win[1][:].indirect(idx_c[:]), COPY)
        g_turn(1, g_first[1], False)
        x_gather_subtract(2, 1)
        x_weigh(2, 1)
        x_gather_second(3, 2)
        x_collect(g_first[1][:], u_bank[:])
        x_turn(2, u_bank[:, 0])
        x_collect(u_late[0][:], u_bank[:, 0:1])
        x_gather_subtract(3, 2)
        x_weigh(3, 2)
        x_turn(3, u_bank[:, 1])
        x_collect(u_late[1][:], u_bank[:, 1:2])
        g_weigh(1)
        x_quantize(0, 2, g_first[1][:])
        quantize(g_codes[1][:], g_scale[1][:], g_in[1])
        x_quantize(2, 3, u_late[0][:])
        x_quantize(3, 4, u_late[1][:])
        for t in range(PACK):
            for h in range(2):
                moment(t, h)

        nc.scalar.copy(out=w_in[0][:].rearrange("p (m t) -> p m t", t=PACK), in_=w_bank[0][:].rearrange("p t m -> p m t"))
        nc.vector.tensor_copy(out=w_in[1][:].rearrange("p (m t) -> p m t", t=PACK), in_=w_bank[1][:].rearrange("p t m -> p m t"))
        for h in range(2):
            quantize(w_codes[h][:], w_scale[h][:], w_in[h][:])
        for h in range(2):
            for half in range(2):
                nc.tensor.matmul_mx(
                    out=v_bank[half],
                    lhsT=dr_codes[:, 2 * P * half : 2 * P * (half + 1)].bitcast(E2M1X4),
                    lhsT_scale=dr_scale[:, P * half : P * (half + 1)],
                    rhs=w_codes[h][:].bitcast(E5M2X4),
                    rhs_scale=w_scale[h][:],
                    start=(h == 0),
                    stop=(h == 1),
                )
        for half in range(2):
            nc.vector.tensor_reduce(
                out=sums[:, half, :],
                in_=v_bank[half].rearrange("p (q e) -> p q e", e=2),
                axis=mybir.AxisListType.X,
                op=ALU.add,
            )
        for half in range(2):
            nc.vector.tensor_scalar(
                result[:, half, :], sums[:, half, :], 0.02, gr_col[:, half : half + 1], ALU.mult, ALU.mult
            )
        nc.sync.dma_start(out=out.rearrange("(a p) q -> p a q", a=2), in_=result[:])
